import numpy as np
import ml_dtypes


def mxq(x, axis, fmt="e4m3"):
    dtype, down = {"e4m3": (ml_dtypes.float8_e4m3fn, 7), "e5m2": (ml_dtypes.float8_e5m2, 14)}[fmt]
    v = np.moveaxis(np.asarray(x, np.float32).astype(ml_dtypes.bfloat16).astype(np.float64), axis, -1)
    blocks = v.reshape(v.shape[:-1] + (-1, 32))
    amax = np.abs(blocks).max(-1, keepdims=True)
    byte = np.maximum(np.where(amax > 0, np.frexp(amax)[1] - 1 + 127, 0) - down, 1)
    scale = np.exp2(byte - 127.0)
    codes = (blocks / scale).astype(np.float32).astype(dtype).astype(np.float64)
    return np.moveaxis((codes * scale).reshape(v.shape), -1, axis)


WIDE = False


def mx_kscale(k):
    if not WIDE:
        return np.ones(k)
    levels = np.array([10, -10, 5, -5, 0])
    if k % 512:
        return np.exp2(np.random.permutation(np.resize(levels, k // 32))).repeat(32)
    a = np.empty((k // 512, 16))
    for p in range(k // 512):
        a[p, :8] = np.random.permutation(np.resize(levels, 8))
        for g in range(8):
            far = levels[np.abs(levels - a[p, g]) >= 10]
            a[p, g + 8] = far[np.random.randint(len(far))]
    return np.exp2(a.ravel()).repeat(32)


def f64(x):
    return np.asarray(x).astype(np.float64)


def striped(idx):
    return np.tile(idx.reshape(-1, 16).T, (8, 1)).astype(np.uint16)


def unstriped(offs):
    return offs[:16].T.reshape(-1).astype(np.int64)


E2M1 = np.array([0.0, 0.5, 1.0, 1.5, 2.0, 3.0, 4.0, 6.0, -0.0, -0.5, -1.0, -1.5, -2.0, -3.0, -4.0, -6.0])


def pack_weight(w, fmt):
    k, n = w.shape
    w = f64(np.asarray(w, np.float32).astype(ml_dtypes.bfloat16)).reshape(k // 32, 32, n)
    amax = np.abs(w).max(1)
    if fmt == "e4m3":
        byte = np.frexp(amax)[1] - 1 + 127 - 7
    else:
        mant, ex = np.frexp(amax / 6.0)
        byte = np.where(mant > 0.5, ex, ex - 1) + 127
    byte = np.clip(np.where(amax > 0, byte, 1), 1, 254)
    scaled = (w * np.exp2(127.0 - byte)[:, None, :]).reshape(k, n).astype(np.float32)
    by_word = np.ascontiguousarray(scaled.reshape(k // 512, 128, 4, n).transpose(0, 1, 3, 2))
    if fmt == "e4m3":
        words = by_word.astype(ml_dtypes.float8_e4m3fn).view(np.uint8)
    else:
        c = by_word.astype(ml_dtypes.float4_e2m1fn).view(np.uint8) & 0xF
        words = (c[..., 0::2] | (c[..., 1::2] << 4)).reshape(k // 512, 128, 2 * n)
    return np.ascontiguousarray(words), np.ascontiguousarray(byte.astype(np.uint8).reshape(k // 512, 16, n))


def unpack_weight(words, scales, fmt):
    g, _, n = scales.shape
    words = np.ascontiguousarray(words).reshape(g, 128, n, -1)
    if fmt == "e4m3":
        vals = words.view(ml_dtypes.float8_e4m3fn).astype(np.float64)
    else:
        nib = np.empty((g, 128, n, 4), np.uint8)
        nib[..., 0::2] = words & 0xF
        nib[..., 1::2] = words >> 4
        vals = E2M1[nib]
    vals = vals * np.repeat(np.exp2(scales.astype(np.float64) - 127.0), 8, axis=1)[..., None]
    return vals.transpose(0, 1, 3, 2).reshape(g * 512, n)


def gelu(v):
    return 0.5 * v * (1.0 + np.tanh(np.sqrt(2.0 / np.pi) * (v + 0.044715 * v**3)))


K, T, E, C, H, N = 1024, 640, 2, 256, 1024, 128


def by_expert(wq, xq):
    return np.concatenate([wq[e].T @ xq[:, e * C:(e + 1) * C] for e in range(E)], axis=1)


def setup_inputs():
    n = np.random.standard_normal
    s = mx_kscale(K)[:, None]
    u = mx_kscale(H)
    w1 = [pack_weight(m, "e2m1") for m in n((E, K, H)) / np.sqrt(K) / s[None]]
    w3 = [pack_weight(m, "e2m1") for m in n((E, K, H)) / np.sqrt(K) / s[None] * u[None, None, :]]
    w2 = [pack_weight(m, "e2m1") for m in n((E, H, N)) / np.sqrt(H) / u[None, :, None]]
    return {
        "xT": (n((K, T)) * s).astype(np.float32),
        "w1_words": np.stack([m[0] for m in w1]),
        "w1_scales": np.stack([m[1] for m in w1]),
        "w3_words": np.stack([m[0] for m in w3]),
        "w3_scales": np.stack([m[1] for m in w3]),
        "w2_words": np.stack([m[0] for m in w2]),
        "w2_scales": np.stack([m[1] for m in w2]),
        "gate": np.tile(np.random.uniform(0.2, 1.0, E * C), (K, 1)).astype(np.float32),
        "offs": striped(np.random.permutation(T)[:E * C]),
    }


def reference(xT, w1_words, w1_scales, w3_words, w3_scales, w2_words, w2_scales, gate, offs):
    idx = unstriped(offs)
    w1 = np.stack([unpack_weight(w1_words[e], w1_scales[e], "e2m1") for e in range(E)])
    w3 = np.stack([unpack_weight(w3_words[e], w3_scales[e], "e2m1") for e in range(E)])
    w2 = np.stack([unpack_weight(w2_words[e], w2_scales[e], "e2m1") for e in range(E)])
    xq = mxq(f64(gate) * f64(xT)[:, idx], 0, "e4m3")
    h = gelu(by_expert(w1, xq))
    h = h * by_expert(w3, xq)
    y = by_expert(w2, mxq(h, 0, "e4m3"))
    out = np.zeros((N, T))
    out[:, idx] = y
    return out

@@ -1,0 +1,306 @@
+from contextlib import ExitStack
+
+import concourse.mybir as mybir
+from concourse.masks import make_identity
+
+K, T, E, C, H, N = 1024, 640, 2, 256, 1024, 128
+FLOPS = 2 * E * C * (2 * K * H + H * N)
+
+F32 = mybir.dt.float32
+BF16 = mybir.dt.bfloat16
+I32 = mybir.dt.int32
+U32 = mybir.dt.uint32
+U16 = mybir.dt.uint16
+U8 = mybir.dt.uint8
+FP8X4 = mybir.dt.float8_e4m3fn_x4
+FP4X4 = mybir.dt.float4_e2m1fn_x4
+MULT = mybir.AluOpType.mult
+ADD = mybir.AluOpType.add
+GELU = mybir.ActivationFunctionType.Gelu_apprx_tanh
+
+P = 128
+PACK = 4
+PASS = P * PACK
+PASSES = K // PASS
+HALVES = H // PASS
+TILE = 128
+TILES_PER_EXPERT = C // TILE
+
+
+def tile_moe_pre_glu_gelu_kernel(
+    tc, xT, w1_words, w1_scales, w3_words, w3_scales, w2_words, w2_scales, gate, offs, out
+):
+    nc = tc.nc
+    with ExitStack() as ctx:
+        keep = ctx.enter_context(tc.tile_pool(name="keep", bufs=1))
+        psum = ctx.enter_context(tc.psum_pool(name="psum", bufs=1))
+
+        first = {"w1": (w1_words, w1_scales), "w3": (w3_words, w3_scales)}
+        x_rows = xT.rearrange("(s p t) w -> s t p w", p=P, t=PACK)
+
+        offsets = keep.tile([P, E * C // 16], U16, name="offsets")
+        zero_in = keep.tile([P, 1], F32, name="zero_in")
+        zero_bias = keep.tile([P, 1], F32, name="zero_bias")
+        ident = keep.tile([P, P], F32, name="ident")
+        window = keep.tile([P, T], F32, name="window")
+        planes = {
+            (m, e): keep.tile([P, PASSES, H], U8, name=f"{m}_plane{e}", align_bytes=64)
+            for m in first
+            for e in range(E)
+        }
+        w2_plane = keep.tile([P, E * HALVES, N], U8, name="w2_plane", align_bytes=64)
+        w2_codes = keep.tile([P, E * HALVES, 2 * N], U8, name="w2_codes", align_bytes=64)
+
+        for e in range(E):
+            for m in first:
+                nc.vector.memset(planes[m, e][:].bitcast(I32), 0)
+        nc.vector.memset(zero_in[:], 0.0)
+        nc.vector.memset(window[:], 0.0)
+        nc.scalar.activation(zero_bias[:], zero_in[:], GELU)
+        nc.gpsimd.memset(w2_plane[:].bitcast(I32), 0)
+        make_identity(nc, ident[:])
+
+        x_planes = {}
+        gates = {}
+        words = {}
+
+        def load_x(s, t):
+            x_planes[s, t] = keep.tile([P, T], F32, name=f"x{s}{t}")
+            nc.sync.dma_start(x_planes[s, t][:], x_rows[s, t])
+
+        def load_gate(e):
+            gates[e] = keep.tile([P, C], F32, name=f"gate{e}", tag=f"gate{e}", align_bytes=64)
+            nc.sync.dma_start(gates[e][:], gate[0:P, e * C : (e + 1) * C])
+
+        def load_scales(m, e, passes, rs):
+            rows = first[m][1][e].rearrange("s (q r) n -> r q s n", r=4)
+            for r in rs:
+                nc.sync.dma_start(planes[m, e][r:P:32, passes].bitcast(I32), rows[r][:, passes].bitcast(I32))
+
+        def load_w2_scales(r):
+            rows = w2_scales.rearrange("e s (q r) n -> r q (e s) n", r=4)
+            nc.gpsimd.dma_start(w2_plane[r:P:32].bitcast(I32), rows[r].bitcast(I32))
+
+        def load_words_of_pass(e, s, ms):
+            for m in ms:
+                codes = keep.tile([P, 2 * H], U8, name=f"{m}_codes{e}_pass{s}", align_bytes=64)
+                nc.sync.dma_start(codes[:].bitcast(I32), first[m][0][e, s].bitcast(I32))
+                for h in range(HALVES):
+                    words[m, e, s, h] = codes[:, 2 * PASS * h : 2 * PASS * (h + 1)]
+
+        def load_words_of_half(e, h, ms):
+            for m in ms:
+                codes = keep.tile([P, PASSES, 2 * PASS], U8, name=f"{m}_codes{e}_half{h}", align_bytes=64)
+                source = first[m][0][e].rearrange("s p n -> p s n")[:, :, 2 * PASS * h : 2 * PASS * (h + 1)]
+                nc.sync.dma_start(codes[:].bitcast(I32), source.bitcast(I32))
+                for s in range(PASSES):
+                    words[m, e, s, h] = codes[:, s, :]
+
+        nc.sync.dma_start(offsets[:], offs)
+        load_x(0, 0)
+        load_gate(0)
+        load_x(0, 1)
+        load_x(0, 2)
+        load_x(0, 3)
+        load_gate(1)
+        pass0, pass1, both = slice(0, 1), slice(1, 2), slice(0, 2)
+        load_scales("w1", 0, pass0, (0, 1))
+        load_words_of_pass(0, 0, ("w1",))
+        load_scales("w1", 0, pass0, (2, 3))
+        load_x(1, 0)
+        load_scales("w3", 0, pass0, (0, 1))
+        load_words_of_pass(0, 0, ("w3",))
+        load_scales("w3", 0, pass0, (2, 3))
+        for t in range(1, PACK):
+            load_x(1, t)
+        for m in first:
+            load_scales(m, 0, pass1, (0, 1))
+            load_words_of_pass(0, 1, (m,))
+            load_scales(m, 0, pass1, (2, 3))
+        nc.sync.dma_start(w2_codes[:].bitcast(I32), w2_words.rearrange("e s p n -> p (e s) n").bitcast(I32))
+        for m in first:
+            load_scales(m, 1, both, (0, 1))
+            load_words_of_half(1, 0, (m,))
+            load_scales(m, 1, both, (2, 3))
+        load_words_of_half(1, 1, first)
+        for r in range(4):
+            load_w2_scales(r)
+
+        gathered = {}
+        x_mx = {}
+
+        def gather(tiles, s, tag):
+            e, c0 = divmod(tiles[0] * TILE, C)
+            width = len(tiles) * TILE
+            values = keep.tile([P, PACK, width], F32, name=f"gathered{tiles[0]}{s}", tag=tag, align_bytes=64)
+            lists = offsets[:, tiles[0] * TILE // 16 : (tiles[0] * TILE + width) // 16]
+            for t in range(PACK):
+                nc.vector.tensor_tensor(
+                    values[:, t, :], x_planes[s, t][:].indirect(lists), gates[e][:, c0 : c0 + width], MULT
+                )
+            for n, j in enumerate(tiles):
+                gathered[j, s] = values[:, :, n * TILE : (n + 1) * TILE]
+
+        def weave(into, j, s):
+            nc.scalar.copy(into, gathered[j, s].rearrange("p t c -> p c t"))
+
+        def weave_on_gpsimd(into, j, s):
+            nc.gpsimd.tensor_scalar(into, gathered[j, s].rearrange("p t c -> p c t"), 1.0, 0.0, MULT, ADD)
+
+        def woven(parts, name, tag):
+            return keep.tile([P, parts, TILE, PACK], BF16, name=name, tag=tag, align_bytes=64)
+
+        def quantize(source, parts, name, tag=None):
+            codes = keep.tile([P, parts, TILE], U32, name=name + "_codes", tag=tag or name + "_codes", align_bytes=64)
+            scales = keep.tile([P, parts, TILE], U8, name=name + "_scales", align_bytes=64)
+            nc.vector.quantize_mx(
+                out=codes[:].rearrange("p g c -> p (g c)").bitcast(FP8X4),
+                scales=scales[:].rearrange("p g c -> p (g c)"),
+                in_=source,
+            )
+            return [(codes[:, g, :], scales[:, g, :]) for g in range(parts)]
+
+        def quantize_x(source, keys, tag=None):
+            made = quantize(source[:].rearrange("p g c t -> p (g c t)"), len(keys), f"x{keys[0][0]}{keys[0][1]}", tag)
+            for key, operand in zip(keys, made):
+                x_mx[key] = operand
+
+        def bank(b, name):
+            return psum.tile([P, PASS], F32, name=name, tag=f"bank{b}")
+
+        sums = {}
+
+        def first_layer(j, h, s, ms):
+            e = j // TILES_PER_EXPERT
+            codes, scales = x_mx[j, s]
+            for m in ms:
+                nc.tensor.matmul_mx(
+                    out=sums[m, j, h][:],
+                    lhsT=codes.bitcast(FP8X4),
+                    lhsT_scale=scales,
+                    rhs=words[m, e, s, h].bitcast(FP4X4),
+                    rhs_scale=planes[m, e][:, s, PASS * h : PASS * (h + 1)],
+                    start=(s == 0),
+                    stop=(s == PASSES - 1),
+                )
+
+        def open_sums(j, h, bank_a, bank_b):
+            sums["w1", j, h] = bank(bank_a, f"a{j}{h}")
+            sums["w3", j, h] = bank(bank_b, f"b{j}{h}")
+
+        def whole_first_layer(j, h, bank_a, bank_b):
+            open_sums(j, h, bank_a, bank_b)
+            for m in first:
+                for s in range(PASSES):
+                    first_layer(j, h, s, (m,))
+
+        hidden = {}
+
+        def in_word_order(ap):
+            return ap.rearrange("c (p u d) -> c u p d", u=2, d=2)
+
+        def activate(j, h):
+            act = keep.tile([P, 2, P, 2], F32, name=f"act{j}{h}", tag=f"act{j}{h}", align_bytes=64)
+            nc.scalar.activation(act[:], in_word_order(sums["w1", j, h][:]), GELU, bias=zero_bias[:])
+            hidden[j, h] = keep.tile([P, 2, P, 2], BF16, name=f"hidden{j}{h}")
+            nc.vector.tensor_tensor(hidden[j, h][:], in_word_order(sums["w3", j, h][:]), act[:], MULT)
+
+        h_words = {}
+        h_mx = {}
+
+        def turn(units, b):
+            turned = bank(b, "turned")[:].rearrange("p (g u c) -> p g u c", u=2, c=TILE)
+            for g, unit in enumerate(units):
+                pairs = hidden[unit][:].rearrange("c u p d -> c (u p d)").bitcast(F32)
+                for u in range(2):
+                    nc.tensor.transpose(turned[:, g, u, :], pairs[:, P * u : P * (u + 1)], ident[:])
+            j, h = units[0]
+            h_words[j, h] = keep.tile([P, len(units), TILE, 2], F32, name=f"h_words{j}{h}", align_bytes=64)
+            nc.scalar.copy(h_words[j, h][:], turned[:, 0 : len(units)].rearrange("p g u c -> p g c u"))
+
+        def quantize_h(units):
+            j, h = units[0]
+            source = h_words[j, h][:].rearrange("p g c u -> p (g c u)").bitcast(BF16)
+            for unit, operand in zip(units, quantize(source, len(units), f"h{j}{h}")):
+                h_mx[unit] = operand
+
+        results = {}
+
+        def second_layer(j, b):
+            e = j // TILES_PER_EXPERT
+            y = bank(b, "y")
+            for h in range(HALVES):
+                codes, scales = h_mx[j, h]
+                nc.tensor.matmul_mx(
+                    out=y[:, 0:TILE],
+                    lhsT=w2_codes[:, e * HALVES + h, :].bitcast(FP4X4),
+                    lhsT_scale=w2_plane[:, e * HALVES + h, :],
+                    rhs=codes.bitcast(FP8X4),
+                    rhs_scale=scales,
+                    start=(h == 0),
+                    stop=(h == HALVES - 1),
+                )
+            results[j] = keep.tile([P, TILE], F32, name=f"result{j}")
+            nc.scalar.copy(results[j][:], y[:, 0:TILE])
+
+        def scatter(j):
+            lists = offsets[:, j * TILE // 16 : (j + 1) * TILE // 16]
+            nc.vector.tensor_copy(window[:].indirect(lists), results[j][:])
+
+        early = [(0, 0), (0, 1), (1, 0), (1, 1)]
+
+        gather((0, 1), 0, "gathered00")
+        for j in (0, 1):
+            x_bf = woven(1, f"x_bf{j}0", f"x_bf{j}0")
+            weave(x_bf[:, 0], j, 0)
+            quantize_x(x_bf, [(j, 0)])
+        for pair, (j, h) in enumerate(early):
+            open_sums(j, h, 2 * pair, 2 * pair + 1)
+            first_layer(j, h, 0, first)
+        gather((0, 1), 1, "gathered01")
+        for j in (0, 1):
+            x_bf = woven(1, f"x_bf{j}1", f"x_bf{j}1")
+            weave(x_bf[:, 0], j, 1)
+            quantize_x(x_bf, [(j, 1)])
+        for j, h in early:
+            first_layer(j, h, 1, first)
+        gather((2, 3), 0, "gathered20")
+        x_bf2 = woven(2, "x_bf2", "x_bf2")
+        x_bf3 = woven(2, "x_bf3", "x_bf3")
+        weave(x_bf2[:, 0], 2, 0)
+        weave(x_bf3[:, 0], 3, 0)
+        gather((2,), 1, "gate0")
+        weave(x_bf2[:, 1], 2, 1)
+        gather((3,), 1, "x_bf01")
+        quantize_x(x_bf2, [(2, 0), (2, 1)])
+        weave_on_gpsimd(x_bf3[:, 1], 3, 1)
+        for j, h in early:
+            activate(j, h)
+        quantize_x(x_bf3, [(3, 0), (3, 1)])
+        whole_first_layer(2, 0, 0, 1)
+        turn(early[0:2], 3)
+        quantize_h(early[0:2])
+        whole_first_layer(2, 1, 4, 5)
+        turn(early[2:4], 7)
+        activate(2, 0)
+        second_layer(0, 2)
+        quantize_h(early[2:4])
+        whole_first_layer(3, 0, 6, 3)
+        activate(2, 1)
+        scatter(0)
+        second_layer(1, 2)
+        whole_first_layer(3, 1, 0, 1)
+        activate(3, 0)
+        turn([(2, 0), (2, 1)], 5)
+        scatter(1)
+        quantize_h([(2, 0), (2, 1)])
+        activate(3, 1)
+        second_layer(2, 2)
+        turn([(3, 0)], 3)
+        quantize_h([(3, 0)])
+        turn([(3, 1)], 1)
+        scatter(2)
+        quantize_h([(3, 1)])
+        second_layer(3, 4)
+        scatter(3)
+        nc.sync.dma_start(out, window[:])

@@ -51,14 +51,11 @@ def tile_moe_pre_glu_gelu_kernel(
         w2_plane = keep.tile([P, E * HALVES, N], U8, name="w2_plane", align_bytes=64)
         w2_codes = keep.tile([P, E * HALVES, 2 * N], U8, name="w2_codes", align_bytes=64)
 
+        nc.vector.memset(zero_in[:], 0.0)
         for e in range(E):
             for m in first:
                 nc.vector.memset(planes[m, e][:].bitcast(I32), 0)
-        nc.vector.memset(zero_in[:], 0.0)
-        nc.vector.memset(window[:], 0.0)
         nc.scalar.activation(zero_bias[:], zero_in[:], GELU)
-        nc.gpsimd.memset(w2_plane[:].bitcast(I32), 0)
-        make_identity(nc, ident[:])
 
         x_planes = {}
         gates = {}
@@ -72,10 +69,10 @@ def tile_moe_pre_glu_gelu_kernel(
             gates[e] = keep.tile([P, C], F32, name=f"gate{e}", tag=f"gate{e}", align_bytes=64)
             nc.sync.dma_start(gates[e][:], gate[0:P, e * C : (e + 1) * C])
 
-        def load_scales(m, e, passes, rs):
+        def load_scales(queue, m, e, rs):
             rows = first[m][1][e].rearrange("s (q r) n -> r q s n", r=4)
             for r in rs:
-                nc.sync.dma_start(planes[m, e][r:P:32, passes].bitcast(I32), rows[r][:, passes].bitcast(I32))
+                queue.dma_start(planes[m, e][r:P:32].bitcast(I32), rows[r].bitcast(I32))
 
         def load_w2_scales(r):
             rows = w2_scales.rearrange("e s (q r) n -> r q (e s) n", r=4)
@@ -103,28 +100,28 @@ def tile_moe_pre_glu_gelu_kernel(
         load_x(0, 2)
         load_x(0, 3)
         load_gate(1)
-        pass0, pass1, both = slice(0, 1), slice(1, 2), slice(0, 2)
-        load_scales("w1", 0, pass0, (0, 1))
         load_words_of_pass(0, 0, ("w1",))
-        load_scales("w1", 0, pass0, (2, 3))
+        load_scales(nc.sync, "w1", 0, range(4))
         load_x(1, 0)
-        load_scales("w3", 0, pass0, (0, 1))
+        load_x(1, 1)
+        load_x(1, 2)
+        load_x(1, 3)
+        load_scales(nc.sync, "w3", 0, range(4))
         load_words_of_pass(0, 0, ("w3",))
-        load_scales("w3", 0, pass0, (2, 3))
-        for t in range(1, PACK):
-            load_x(1, t)
-        for m in first:
-            load_scales(m, 0, pass1, (0, 1))
-            load_words_of_pass(0, 1, (m,))
-            load_scales(m, 0, pass1, (2, 3))
+        load_words_of_pass(0, 1, ("w1",))
+        load_words_of_pass(0, 1, ("w3",))
+        load_scales(nc.sync, "w1", 1, range(4))
+        load_words_of_half(1, 0, ("w1",))
+        load_scales(nc.sync, "w3", 1, range(4))
+        load_words_of_half(1, 0, ("w3",))
+        load_words_of_half(1, 1, ("w1",))
+        load_words_of_half(1, 1, ("w3",))
         nc.sync.dma_start(w2_codes[:].bitcast(I32), w2_words.rearrange("e s p n -> p (e s) n").bitcast(I32))
-        for m in first:
-            load_scales(m, 1, both, (0, 1))
-            load_words_of_half(1, 0, (m,))
-            load_scales(m, 1, both, (2, 3))
-        load_words_of_half(1, 1, first)
+        make_identity(nc, ident[:])
+        nc.gpsimd.memset(w2_plane[:].bitcast(I32), 0)
         for r in range(4):
             load_w2_scales(r)
+        nc.gpsimd.memset(window[:], 0.0)
 
         gathered = {}
         x_mx = {}
@@ -142,10 +139,19 @@ def tile_moe_pre_glu_gelu_kernel(
                 gathered[j, s] = values[:, :, n * TILE : (n + 1) * TILE]
 
         def weave(into, j, s):
-            nc.scalar.copy(into, gathered[j, s].rearrange("p t c -> p c t"))
+            nc.scalar.copy(
+                into.rearrange("p (c i) t -> p c t i", i=4),
+                gathered[j, s].rearrange("p t (c i) -> p c t i", i=4),
+            )
 
         def weave_on_gpsimd(into, j, s):
             nc.gpsimd.tensor_scalar(into, gathered[j, s].rearrange("p t c -> p c t"), 1.0, 0.0, MULT, ADD)
+
+        def weave_on_vector(into, j, s):
+            nc.vector.tensor_copy(
+                into.rearrange("p (c i) t -> p c t i", i=4),
+                gathered[j, s].rearrange("p t (c i) -> p c t i", i=4),
+            )
 
         def woven(parts, name, tag):
             return keep.tile([P, parts, TILE, PACK], BF16, name=name, tag=tag, align_bytes=64)
@@ -256,7 +262,9 @@ def tile_moe_pre_glu_gelu_kernel(
             quantize_x(x_bf, [(j, 0)])
         for pair, (j, h) in enumerate(early):
             open_sums(j, h, 2 * pair, 2 * pair + 1)
-            first_layer(j, h, 0, first)
+        for m in first:
+            for j, h in early:
+                first_layer(j, h, 0, (m,))
         gather((0, 1), 1, "gathered01")
         for j in (0, 1):
             x_bf = woven(1, f"x_bf{j}1", f"x_bf{j}1")
@@ -264,18 +272,20 @@ def tile_moe_pre_glu_gelu_kernel(
             quantize_x(x_bf, [(j, 1)])
         for j, h in early:
             first_layer(j, h, 1, first)
-        gather((2, 3), 0, "gathered20")
         x_bf2 = woven(2, "x_bf2", "x_bf2")
         x_bf3 = woven(2, "x_bf3", "x_bf3")
+        gather((2, 3), 0, "gathered20")
         weave(x_bf2[:, 0], 2, 0)
         weave(x_bf3[:, 0], 3, 0)
         gather((2,), 1, "gate0")
         weave(x_bf2[:, 1], 2, 1)
-        gather((3,), 1, "x_bf01")
         quantize_x(x_bf2, [(2, 0), (2, 1)])
-        weave_on_gpsimd(x_bf3[:, 1], 3, 1)
-        for j, h in early:
-            activate(j, h)
+        activate(0, 0)
+        activate(0, 1)
+        gather((3,), 1, "x_bf11")
+        activate(1, 0)
+        activate(1, 1)
+        weave(x_bf3[:, 1], 3, 1)
         quantize_x(x_bf3, [(3, 0), (3, 1)])
         whole_first_layer(2, 0, 0, 1)
         turn(early[0:2], 3)

@@ -65,9 +65,9 @@ def tile_moe_pre_glu_gelu_kernel(
             x_planes[s, t] = keep.tile([P, T], F32, name=f"x{s}{t}")
             nc.sync.dma_start(x_planes[s, t][:], x_rows[s, t])
 
-        def load_gate(e):
-            gates[e] = keep.tile([P, C], F32, name=f"gate{e}", tag=f"gate{e}", align_bytes=64)
-            nc.sync.dma_start(gates[e][:], gate[0:P, e * C : (e + 1) * C])
+        def load_gate(tiles):
+            gates[tiles] = keep.tile([P, len(tiles) * TILE], F32, name=f"gate{tiles[0]}", align_bytes=64)
+            nc.sync.dma_start(gates[tiles][:], gate[0:P, tiles[0] * TILE : (tiles[-1] + 1) * TILE])
 
         def load_scales(queue, m, e, rs):
             rows = first[m][1][e].rearrange("s (q r) n -> r q s n", r=4)
@@ -85,6 +85,13 @@ def tile_moe_pre_glu_gelu_kernel(
                 for h in range(HALVES):
                     words[m, e, s, h] = codes[:, 2 * PASS * h : 2 * PASS * (h + 1)]
 
+        def load_words_of_expert(e, m):
+            codes = keep.tile([P, PASSES, 2 * H], U8, name=f"{m}_codes{e}", align_bytes=64)
+            nc.sync.dma_start(codes[:].bitcast(I32), first[m][0][e].rearrange("s p n -> p s n").bitcast(I32))
+            for s in range(PASSES):
+                for h in range(HALVES):
+                    words[m, e, s, h] = codes[:, s, 2 * PASS * h : 2 * PASS * (h + 1)]
+
         def load_words_of_half(e, h, ms):
             for m in ms:
                 codes = keep.tile([P, PASSES, 2 * PASS], U8, name=f"{m}_codes{e}_half{h}", align_bytes=64)
@@ -93,29 +100,27 @@ def tile_moe_pre_glu_gelu_kernel(
                 for s in range(PASSES):
                     words[m, e, s, h] = codes[:, s, :]
 
-        nc.sync.dma_start(offsets[:], offs)
         load_x(0, 0)
-        load_gate(0)
+        load_gate((0, 1))
+        nc.sync.dma_start(offsets[:], offs)
         load_x(0, 1)
         load_x(0, 2)
         load_x(0, 3)
-        load_gate(1)
-        load_words_of_pass(0, 0, ("w1",))
-        load_scales(nc.sync, "w1", 0, range(4))
+        load_gate((2, 3))
         load_x(1, 0)
         load_x(1, 1)
+        load_words_of_pass(0, 0, ("w1",))
         load_x(1, 2)
+        load_scales(nc.sync, "w1", 0, range(4))
         load_x(1, 3)
         load_scales(nc.sync, "w3", 0, range(4))
         load_words_of_pass(0, 0, ("w3",))
         load_words_of_pass(0, 1, ("w1",))
         load_words_of_pass(0, 1, ("w3",))
         load_scales(nc.sync, "w1", 1, range(4))
-        load_words_of_half(1, 0, ("w1",))
+        load_words_of_expert(1, "w1")
         load_scales(nc.sync, "w3", 1, range(4))
-        load_words_of_half(1, 0, ("w3",))
-        load_words_of_half(1, 1, ("w1",))
-        load_words_of_half(1, 1, ("w3",))
+        load_words_of_expert(1, "w3")
         nc.sync.dma_start(w2_codes[:].bitcast(I32), w2_words.rearrange("e s p n -> p (e s) n").bitcast(I32))
         make_identity(nc, ident[:])
         nc.gpsimd.memset(w2_plane[:].bitcast(I32), 0)
@@ -126,23 +131,24 @@ def tile_moe_pre_glu_gelu_kernel(
         gathered = {}
         x_mx = {}
 
+        def gate_of(tiles):
+            held = [key for key in gates if tiles[0] in key][0]
+            c0 = (tiles[0] - held[0]) * TILE
+            return gates[held][:, c0 : c0 + len(tiles) * TILE]
+
         def gather(tiles, s, tag):
-            e, c0 = divmod(tiles[0] * TILE, C)
             width = len(tiles) * TILE
             values = keep.tile([P, PACK, width], F32, name=f"gathered{tiles[0]}{s}", tag=tag, align_bytes=64)
             lists = offsets[:, tiles[0] * TILE // 16 : (tiles[0] * TILE + width) // 16]
             for t in range(PACK):
                 nc.vector.tensor_tensor(
-                    values[:, t, :], x_planes[s, t][:].indirect(lists), gates[e][:, c0 : c0 + width], MULT
+                    values[:, t, :], x_planes[s, t][:].indirect(lists), gate_of(tiles), MULT
                 )
             for n, j in enumerate(tiles):
                 gathered[j, s] = values[:, :, n * TILE : (n + 1) * TILE]
 
         def weave(into, j, s):
-            nc.scalar.copy(
-                into.rearrange("p (c i) t -> p c t i", i=4),
-                gathered[j, s].rearrange("p t (c i) -> p c t i", i=4),
-            )
+            nc.scalar.copy(into, gathered[j, s].rearrange("p t c -> p c t"))
 
         def weave_on_gpsimd(into, j, s):
             nc.gpsimd.tensor_scalar(into, gathered[j, s].rearrange("p t c -> p c t"), 1.0, 0.0, MULT, ADD)
@@ -273,20 +279,22 @@ def tile_moe_pre_glu_gelu_kernel(
         for j, h in early:
             first_layer(j, h, 1, first)
         x_bf2 = woven(2, "x_bf2", "x_bf2")
-        x_bf3 = woven(2, "x_bf3", "x_bf3")
+        x_bf30 = woven(1, "x_bf30", "x_bf30")
         gather((2, 3), 0, "gathered20")
         weave(x_bf2[:, 0], 2, 0)
-        weave(x_bf3[:, 0], 3, 0)
+        weave(x_bf30[:, 0], 3, 0)
         gather((2,), 1, "gate0")
         weave(x_bf2[:, 1], 2, 1)
         quantize_x(x_bf2, [(2, 0), (2, 1)])
+        gather((3,), 1, "x_bf01")
+        quantize_x(x_bf30, [(3, 0)], "x_bf11")
         activate(0, 0)
         activate(0, 1)
-        gather((3,), 1, "x_bf11")
         activate(1, 0)
+        x_bf31 = woven(1, "x_bf31", "act00")
+        weave(x_bf31[:, 0], 3, 1)
         activate(1, 1)
-        weave(x_bf3[:, 1], 3, 1)
-        quantize_x(x_bf3, [(3, 0), (3, 1)])
+        quantize_x(x_bf31, [(3, 1)])
         whole_first_layer(2, 0, 0, 1)
         turn(early[0:2], 3)
         quantize_h(early[0:2])
@@ -299,9 +307,9 @@ def tile_moe_pre_glu_gelu_kernel(
         activate(2, 1)
         scatter(0)
         second_layer(1, 2)
+        turn([(2, 0), (2, 1)], 5)
         whole_first_layer(3, 1, 0, 1)
         activate(3, 0)
-        turn([(2, 0), (2, 1)], 5)
         scatter(1)
         quantize_h([(2, 0), (2, 1)])
         activate(3, 1)

@@ -52,10 +52,13 @@ def tile_moe_pre_glu_gelu_kernel(
         w2_codes = keep.tile([P, E * HALVES, 2 * N], U8, name="w2_codes", align_bytes=64)
 
         nc.vector.memset(zero_in[:], 0.0)
-        for e in range(E):
+        for e in reversed(range(E)):
             for m in first:
                 nc.vector.memset(planes[m, e][:].bitcast(I32), 0)
+        nc.gpsimd.memset(w2_plane[:].bitcast(I32), 0)
+        nc.gpsimd.memset(window[:], 0.0)
         nc.scalar.activation(zero_bias[:], zero_in[:], GELU)
+        make_identity(nc, ident[:])
 
         x_planes = {}
         gates = {}
@@ -69,14 +72,25 @@ def tile_moe_pre_glu_gelu_kernel(
             gates[tiles] = keep.tile([P, len(tiles) * TILE], F32, name=f"gate{tiles[0]}", align_bytes=64)
             nc.sync.dma_start(gates[tiles][:], gate[0:P, tiles[0] * TILE : (tiles[-1] + 1) * TILE])
 
+        def spread_gate(tiles, b):
+            count = len(tiles)
+            column = keep.tile([P, count], F32, name="gate_column")
+            row = gate[0, tiles[0] * TILE : (tiles[-1] + 1) * TILE]
+            nc.sync.dma_start(column[:], row.rearrange("(p c) -> p c", c=count))
+            spread = psum.tile([P, count, P], F32, name="spread", tag=f"bank{b}")
+            for c in range(count):
+                nc.tensor.transpose(spread[:, c, :], column[:, c : c + 1].to_broadcast([P, P]), ident[:])
+            gates[tiles] = keep.tile([P, count * TILE], F32, name=f"gate{tiles[0]}", align_bytes=64)
+            nc.scalar.copy(gates[tiles][:].rearrange("f (p c) -> f p c", c=count), spread[:].rearrange("f c p -> f p c"))
+
         def load_scales(queue, m, e, rs):
             rows = first[m][1][e].rearrange("s (q r) n -> r q s n", r=4)
             for r in rs:
                 queue.dma_start(planes[m, e][r:P:32].bitcast(I32), rows[r].bitcast(I32))
 
-        def load_w2_scales(r):
+        def load_w2_scales(queue, r):
             rows = w2_scales.rearrange("e s (q r) n -> r q (e s) n", r=4)
-            nc.gpsimd.dma_start(w2_plane[r:P:32].bitcast(I32), rows[r].bitcast(I32))
+            queue.dma_start(w2_plane[r:P:32].bitcast(I32), rows[r].bitcast(I32))
 
         def load_words_of_pass(e, s, ms):
             for m in ms:
@@ -103,30 +117,27 @@ def tile_moe_pre_glu_gelu_kernel(
         load_x(0, 0)
         load_gate((0, 1))
         nc.sync.dma_start(offsets[:], offs)
+        spread_gate((2, 3), 7)
         load_x(0, 1)
         load_x(0, 2)
         load_x(0, 3)
-        load_gate((2, 3))
         load_x(1, 0)
         load_x(1, 1)
         load_words_of_pass(0, 0, ("w1",))
         load_x(1, 2)
-        load_scales(nc.sync, "w1", 0, range(4))
         load_x(1, 3)
+        load_scales(nc.sync, "w1", 0, range(4))
         load_scales(nc.sync, "w3", 0, range(4))
         load_words_of_pass(0, 0, ("w3",))
         load_words_of_pass(0, 1, ("w1",))
         load_words_of_pass(0, 1, ("w3",))
-        load_scales(nc.sync, "w1", 1, range(4))
         load_words_of_expert(1, "w1")
-        load_scales(nc.sync, "w3", 1, range(4))
         load_words_of_expert(1, "w3")
         nc.sync.dma_start(w2_codes[:].bitcast(I32), w2_words.rearrange("e s p n -> p (e s) n").bitcast(I32))
-        make_identity(nc, ident[:])
-        nc.gpsimd.memset(w2_plane[:].bitcast(I32), 0)
         for r in range(4):
-            load_w2_scales(r)
-        nc.gpsimd.memset(window[:], 0.0)
+            load_w2_scales(nc.sync, r)
+        load_scales(nc.gpsimd, "w1", 1, range(4))
+        load_scales(nc.gpsimd, "w3", 1, range(4))
 
         gathered = {}
         x_mx = {}
@@ -206,16 +217,25 @@ def tile_moe_pre_glu_gelu_kernel(
                 for s in range(PASSES):
                     first_layer(j, h, s, (m,))
 
+        def both_passes(j, h, m, b):
+            sums[m, j, h] = bank(b, f"{m}_sum{j}{h}")
+            for s in range(PASSES):
+                first_layer(j, h, s, (m,))
+
         hidden = {}
 
         def in_word_order(ap):
             return ap.rearrange("c (p u d) -> c u p d", u=2, d=2)
 
-        def activate(j, h):
+        def activate(j, h, split=False):
             act = keep.tile([P, 2, P, 2], F32, name=f"act{j}{h}", tag=f"act{j}{h}", align_bytes=64)
             nc.scalar.activation(act[:], in_word_order(sums["w1", j, h][:]), GELU, bias=zero_bias[:])
             hidden[j, h] = keep.tile([P, 2, P, 2], BF16, name=f"hidden{j}{h}")
-            nc.vector.tensor_tensor(hidden[j, h][:], in_word_order(sums["w3", j, h][:]), act[:], MULT)
+            if split:
+                for u in range(2):
+                    nc.vector.tensor_tensor(hidden[j, h][:, u], in_word_order(sums["w3", j, h][:])[:, u], act[:, u], MULT)
+            else:
+                nc.vector.tensor_tensor(hidden[j, h][:], in_word_order(sums["w3", j, h][:]), act[:], MULT)
 
         h_words = {}
         h_mx = {}
@@ -295,30 +315,34 @@ def tile_moe_pre_glu_gelu_kernel(
         weave(x_bf31[:, 0], 3, 1)
         activate(1, 1)
         quantize_x(x_bf31, [(3, 1)])
-        whole_first_layer(2, 0, 0, 1)
-        turn(early[0:2], 3)
-        quantize_h(early[0:2])
-        whole_first_layer(2, 1, 4, 5)
-        turn(early[2:4], 7)
+        both_passes(2, 0, "w1", 0)
+        both_passes(2, 1, "w1", 2)
+        both_passes(2, 0, "w3", 1)
+        both_passes(2, 1, "w3", 3)
         activate(2, 0)
-        second_layer(0, 2)
-        quantize_h(early[2:4])
-        whole_first_layer(3, 0, 6, 3)
+        turn(early[0:2], 0)
+        both_passes(3, 0, "w1", 4)
         activate(2, 1)
-        scatter(0)
-        second_layer(1, 2)
-        turn([(2, 0), (2, 1)], 5)
-        whole_first_layer(3, 1, 0, 1)
+        both_passes(3, 0, "w3", 5)
+        quantize_h(early[0:2])
+        turn(early[2:4], 2)
+        both_passes(3, 1, "w1", 6)
         activate(3, 0)
-        scatter(1)
-        quantize_h([(2, 0), (2, 1)])
+        both_passes(3, 1, "w3", 7)
+        second_layer(0, 1)
         activate(3, 1)
-        second_layer(2, 2)
-        turn([(3, 0)], 3)
+        quantize_h(early[2:4])
+        turn([(2, 0), (2, 1)], 3)
+        scatter(0)
+        second_layer(1, 4)
+        quantize_h([(2, 0), (2, 1)])
+        turn([(3, 0)], 5)
+        turn([(3, 1)], 7)
+        second_layer(2, 6)
+        scatter(1)
         quantize_h([(3, 0)])
-        turn([(3, 1)], 1)
-        scatter(2)
         quantize_h([(3, 1)])
-        second_layer(3, 4)
+        scatter(2)
+        second_layer(3, 0)
         scatter(3)
         nc.sync.dma_start(out, window[:])

@@ -15,7 +15,6 @@ U8 = mybir.dt.uint8
 FP8X4 = mybir.dt.float8_e4m3fn_x4
 FP4X4 = mybir.dt.float4_e2m1fn_x4
 MULT = mybir.AluOpType.mult
-ADD = mybir.AluOpType.add
 GELU = mybir.ActivationFunctionType.Gelu_apprx_tanh
 
 P = 128
@@ -25,6 +24,11 @@ PASSES = K // PASS
 HALVES = H // PASS
 TILE = 128
 TILES_PER_EXPERT = C // TILE
+QUADRANT = 32
+SCALE_ROWS = 4
+FP4_BYTES = 2
+PER_COLUMN = 16
+ALIGN = 64
 
 
 def tile_moe_pre_glu_gelu_kernel(
@@ -38,27 +42,30 @@ def tile_moe_pre_glu_gelu_kernel(
         first = {"w1": (w1_words, w1_scales), "w3": (w3_words, w3_scales)}
         x_rows = xT.rearrange("(s p t) w -> s t p w", p=P, t=PACK)
 
-        offsets = keep.tile([P, E * C // 16], U16, name="offsets")
+        offsets = keep.tile([P, E * C // PER_COLUMN], U16, name="offsets")
         zero_in = keep.tile([P, 1], F32, name="zero_in")
         zero_bias = keep.tile([P, 1], F32, name="zero_bias")
         ident = keep.tile([P, P], F32, name="ident")
         window = keep.tile([P, T], F32, name="window")
         planes = {
-            (m, e): keep.tile([P, PASSES, H], U8, name=f"{m}_plane{e}", align_bytes=64)
+            (m, e): keep.tile([P, PASSES, H], U8, name=f"{m}_plane{e}", align_bytes=ALIGN)
             for m in first
             for e in range(E)
         }
-        w2_plane = keep.tile([P, E * HALVES, N], U8, name="w2_plane", align_bytes=64)
-        w2_codes = keep.tile([P, E * HALVES, 2 * N], U8, name="w2_codes", align_bytes=64)
+        w2_plane = keep.tile([P, E * HALVES, N], U8, name="w2_plane", align_bytes=ALIGN)
+        w2_codes = keep.tile([P, E * HALVES, FP4_BYTES * N], U8, name="w2_codes", align_bytes=ALIGN)
 
         nc.vector.memset(zero_in[:], 0.0)
         for e in reversed(range(E)):
             for m in first:
                 nc.vector.memset(planes[m, e][:].bitcast(I32), 0)
+        make_identity(nc, ident[:])
         nc.gpsimd.memset(w2_plane[:].bitcast(I32), 0)
         nc.gpsimd.memset(window[:], 0.0)
         nc.scalar.activation(zero_bias[:], zero_in[:], GELU)
-        make_identity(nc, ident[:])
+
+        def bank(b, name):
+            return psum.tile([P, PASS], F32, name=name, tag=f"bank{b}")
 
         x_planes = {}
         gates = {}
@@ -68,114 +75,93 @@ def tile_moe_pre_glu_gelu_kernel(
             x_planes[s, t] = keep.tile([P, T], F32, name=f"x{s}{t}")
             nc.sync.dma_start(x_planes[s, t][:], x_rows[s, t])
 
-        def load_gate(tiles):
-            gates[tiles] = keep.tile([P, len(tiles) * TILE], F32, name=f"gate{tiles[0]}", align_bytes=64)
-            nc.sync.dma_start(gates[tiles][:], gate[0:P, tiles[0] * TILE : (tiles[-1] + 1) * TILE])
+        def load_gate(e):
+            gates[e] = keep.tile([P, C], F32, name=f"gate{e * TILES_PER_EXPERT}", align_bytes=ALIGN)
+            nc.sync.dma_start(gates[e][:], gate[0:P, e * C : (e + 1) * C])
 
-        def spread_gate(tiles, b):
-            count = len(tiles)
-            column = keep.tile([P, count], F32, name="gate_column")
-            row = gate[0, tiles[0] * TILE : (tiles[-1] + 1) * TILE]
-            nc.sync.dma_start(column[:], row.rearrange("(p c) -> p c", c=count))
-            spread = psum.tile([P, count, P], F32, name="spread", tag=f"bank{b}")
-            for c in range(count):
+        def spread_gate(e, b):
+            column = keep.tile([P, TILES_PER_EXPERT], F32, name="gate_column")
+            row = gate[0, e * C : (e + 1) * C]
+            nc.sync.dma_start(column[:], row.rearrange("(p c) -> p c", c=TILES_PER_EXPERT))
+            spread = psum.tile([P, TILES_PER_EXPERT, P], F32, name="spread", tag=f"bank{b}")
+            for c in range(TILES_PER_EXPERT):
                 nc.tensor.transpose(spread[:, c, :], column[:, c : c + 1].to_broadcast([P, P]), ident[:])
-            gates[tiles] = keep.tile([P, count * TILE], F32, name=f"gate{tiles[0]}", align_bytes=64)
-            nc.scalar.copy(gates[tiles][:].rearrange("f (p c) -> f p c", c=count), spread[:].rearrange("f c p -> f p c"))
+            gates[e] = keep.tile([P, C], F32, name=f"gate{e * TILES_PER_EXPERT}", align_bytes=ALIGN)
+            nc.scalar.copy(
+                gates[e][:].rearrange("f (p c) -> f p c", c=TILES_PER_EXPERT), spread[:].rearrange("f c p -> f p c")
+            )
 
-        def load_scales(queue, m, e, rs):
-            rows = first[m][1][e].rearrange("s (q r) n -> r q s n", r=4)
-            for r in rs:
-                queue.dma_start(planes[m, e][r:P:32].bitcast(I32), rows[r].bitcast(I32))
+        def load_scales(queue, plane, rows):
+            for r in range(SCALE_ROWS):
+                queue.dma_start(plane[r:P:QUADRANT].bitcast(I32), rows[r].bitcast(I32))
 
-        def load_w2_scales(queue, r):
-            rows = w2_scales.rearrange("e s (q r) n -> r q (e s) n", r=4)
-            queue.dma_start(w2_plane[r:P:32].bitcast(I32), rows[r].bitcast(I32))
+        def load_first_scales(queue, m, e):
+            load_scales(queue, planes[m, e], first[m][1][e].rearrange("s (q r) n -> r q s n", r=SCALE_ROWS))
 
-        def load_words_of_pass(e, s, ms):
-            for m in ms:
-                codes = keep.tile([P, 2 * H], U8, name=f"{m}_codes{e}_pass{s}", align_bytes=64)
-                nc.sync.dma_start(codes[:].bitcast(I32), first[m][0][e, s].bitcast(I32))
-                for h in range(HALVES):
-                    words[m, e, s, h] = codes[:, 2 * PASS * h : 2 * PASS * (h + 1)]
+        def half_bytes(h):
+            return slice(FP4_BYTES * PASS * h, FP4_BYTES * PASS * (h + 1))
 
-        def load_words_of_expert(e, m):
-            codes = keep.tile([P, PASSES, 2 * H], U8, name=f"{m}_codes{e}", align_bytes=64)
+        def load_words_of_pass(m, e, s):
+            codes = keep.tile([P, FP4_BYTES * H], U8, name=f"{m}_codes{e}_pass{s}", align_bytes=ALIGN)
+            nc.sync.dma_start(codes[:].bitcast(I32), first[m][0][e, s].bitcast(I32))
+            for h in range(HALVES):
+                words[m, e, s, h] = codes[:, half_bytes(h)]
+
+        def load_words_of_expert(m, e):
+            codes = keep.tile([P, PASSES, FP4_BYTES * H], U8, name=f"{m}_codes{e}", align_bytes=ALIGN)
             nc.sync.dma_start(codes[:].bitcast(I32), first[m][0][e].rearrange("s p n -> p s n").bitcast(I32))
             for s in range(PASSES):
                 for h in range(HALVES):
-                    words[m, e, s, h] = codes[:, s, 2 * PASS * h : 2 * PASS * (h + 1)]
-
-        def load_words_of_half(e, h, ms):
-            for m in ms:
-                codes = keep.tile([P, PASSES, 2 * PASS], U8, name=f"{m}_codes{e}_half{h}", align_bytes=64)
-                source = first[m][0][e].rearrange("s p n -> p s n")[:, :, 2 * PASS * h : 2 * PASS * (h + 1)]
-                nc.sync.dma_start(codes[:].bitcast(I32), source.bitcast(I32))
-                for s in range(PASSES):
-                    words[m, e, s, h] = codes[:, s, :]
+                    words[m, e, s, h] = codes[:, s, half_bytes(h)]
 
         load_x(0, 0)
-        load_gate((0, 1))
+        load_gate(0)
         nc.sync.dma_start(offsets[:], offs)
-        spread_gate((2, 3), 7)
-        load_x(0, 1)
-        load_x(0, 2)
-        load_x(0, 3)
-        load_x(1, 0)
-        load_x(1, 1)
-        load_words_of_pass(0, 0, ("w1",))
-        load_x(1, 2)
-        load_x(1, 3)
-        load_scales(nc.sync, "w1", 0, range(4))
-        load_scales(nc.sync, "w3", 0, range(4))
-        load_words_of_pass(0, 0, ("w3",))
-        load_words_of_pass(0, 1, ("w1",))
-        load_words_of_pass(0, 1, ("w3",))
-        load_words_of_expert(1, "w1")
-        load_words_of_expert(1, "w3")
+        spread_gate(1, 7)
+        for t in range(1, PACK):
+            load_x(0, t)
+        for t in range(PACK // 2):
+            load_x(1, t)
+        load_words_of_pass("w1", 0, 0)
+        for t in range(PACK // 2, PACK):
+            load_x(1, t)
+        for m in first:
+            load_first_scales(nc.sync, m, 0)
+        load_words_of_pass("w3", 0, 0)
+        for m in first:
+            load_words_of_pass(m, 0, 1)
+        for m in first:
+            load_words_of_expert(m, 1)
         nc.sync.dma_start(w2_codes[:].bitcast(I32), w2_words.rearrange("e s p n -> p (e s) n").bitcast(I32))
-        for r in range(4):
-            load_w2_scales(nc.sync, r)
-        load_scales(nc.gpsimd, "w1", 1, range(4))
-        load_scales(nc.gpsimd, "w3", 1, range(4))
+        load_scales(nc.sync, w2_plane, w2_scales.rearrange("e s (q r) n -> r q (e s) n", r=SCALE_ROWS))
+        for m in first:
+            load_first_scales(nc.gpsimd, m, 1)
+
+        def list_of(tiles):
+            return offsets[:, tiles[0] * TILE // PER_COLUMN : (tiles[-1] + 1) * TILE // PER_COLUMN]
 
         gathered = {}
-        x_mx = {}
-
-        def gate_of(tiles):
-            held = [key for key in gates if tiles[0] in key][0]
-            c0 = (tiles[0] - held[0]) * TILE
-            return gates[held][:, c0 : c0 + len(tiles) * TILE]
 
         def gather(tiles, s, tag):
+            e, c0 = divmod(tiles[0] * TILE, C)
             width = len(tiles) * TILE
-            values = keep.tile([P, PACK, width], F32, name=f"gathered{tiles[0]}{s}", tag=tag, align_bytes=64)
-            lists = offsets[:, tiles[0] * TILE // 16 : (tiles[0] * TILE + width) // 16]
+            values = keep.tile([P, PACK, width], F32, name=f"gathered{tiles[0]}{s}", tag=tag, align_bytes=ALIGN)
             for t in range(PACK):
                 nc.vector.tensor_tensor(
-                    values[:, t, :], x_planes[s, t][:].indirect(lists), gate_of(tiles), MULT
+                    values[:, t, :], x_planes[s, t][:].indirect(list_of(tiles)), gates[e][:, c0 : c0 + width], MULT
                 )
             for n, j in enumerate(tiles):
                 gathered[j, s] = values[:, :, n * TILE : (n + 1) * TILE]
 
+        def woven(parts, name, tag):
+            return keep.tile([P, parts, TILE, PACK], BF16, name=name, tag=tag, align_bytes=ALIGN)
+
         def weave(into, j, s):
             nc.scalar.copy(into, gathered[j, s].rearrange("p t c -> p c t"))
 
-        def weave_on_gpsimd(into, j, s):
-            nc.gpsimd.tensor_scalar(into, gathered[j, s].rearrange("p t c -> p c t"), 1.0, 0.0, MULT, ADD)
-
-        def weave_on_vector(into, j, s):
-            nc.vector.tensor_copy(
-                into.rearrange("p (c i) t -> p c t i", i=4),
-                gathered[j, s].rearrange("p t (c i) -> p c t i", i=4),
-            )
-
-        def woven(parts, name, tag):
-            return keep.tile([P, parts, TILE, PACK], BF16, name=name, tag=tag, align_bytes=64)
-
-        def quantize(source, parts, name, tag=None):
-            codes = keep.tile([P, parts, TILE], U32, name=name + "_codes", tag=tag or name + "_codes", align_bytes=64)
-            scales = keep.tile([P, parts, TILE], U8, name=name + "_scales", align_bytes=64)
+        def quantize(source, parts, name, tag):
+            codes = keep.tile([P, parts, TILE], U32, name=name + "_codes", tag=tag, align_bytes=ALIGN)
+            scales = keep.tile([P, parts, TILE], U8, name=name + "_scales", align_bytes=ALIGN)
             nc.vector.quantize_mx(
                 out=codes[:].rearrange("p g c -> p (g c)").bitcast(FP8X4),
                 scales=scales[:].rearrange("p g c -> p (g c)"),
@@ -183,78 +169,62 @@ def tile_moe_pre_glu_gelu_kernel(
             )
             return [(codes[:, g, :], scales[:, g, :]) for g in range(parts)]
 
-        def quantize_x(source, keys, tag=None):
-            made = quantize(source[:].rearrange("p g c t -> p (g c t)"), len(keys), f"x{keys[0][0]}{keys[0][1]}", tag)
-            for key, operand in zip(keys, made):
-                x_mx[key] = operand
+        x_mx = {}
 
-        def bank(b, name):
-            return psum.tile([P, PASS], F32, name=name, tag=f"bank{b}")
+        def quantize_x(source, j, passes, tag):
+            flat = source[:].rearrange("p g c t -> p (g c t)")
+            for s, operand in zip(passes, quantize(flat, len(passes), f"x{j}{passes[0]}", tag)):
+                x_mx[j, s] = operand
 
         sums = {}
 
-        def first_layer(j, h, s, ms):
+        def first_layer(j, h, s, m):
             e = j // TILES_PER_EXPERT
             codes, scales = x_mx[j, s]
-            for m in ms:
-                nc.tensor.matmul_mx(
-                    out=sums[m, j, h][:],
-                    lhsT=codes.bitcast(FP8X4),
-                    lhsT_scale=scales,
-                    rhs=words[m, e, s, h].bitcast(FP4X4),
-                    rhs_scale=planes[m, e][:, s, PASS * h : PASS * (h + 1)],
-                    start=(s == 0),
-                    stop=(s == PASSES - 1),
-                )
-
-        def open_sums(j, h, bank_a, bank_b):
-            sums["w1", j, h] = bank(bank_a, f"a{j}{h}")
-            sums["w3", j, h] = bank(bank_b, f"b{j}{h}")
-
-        def whole_first_layer(j, h, bank_a, bank_b):
-            open_sums(j, h, bank_a, bank_b)
-            for m in first:
-                for s in range(PASSES):
-                    first_layer(j, h, s, (m,))
+            nc.tensor.matmul_mx(
+                out=sums[m, j, h][:],
+                lhsT=codes.bitcast(FP8X4),
+                lhsT_scale=scales,
+                rhs=words[m, e, s, h].bitcast(FP4X4),
+                rhs_scale=planes[m, e][:, s, PASS * h : PASS * (h + 1)],
+                start=(s == 0),
+                stop=(s == PASSES - 1),
+            )
 
         def both_passes(j, h, m, b):
             sums[m, j, h] = bank(b, f"{m}_sum{j}{h}")
             for s in range(PASSES):
-                first_layer(j, h, s, (m,))
+                first_layer(j, h, s, m)
 
         hidden = {}
 
         def in_word_order(ap):
             return ap.rearrange("c (p u d) -> c u p d", u=2, d=2)
 
-        def activate(j, h, split=False):
-            act = keep.tile([P, 2, P, 2], F32, name=f"act{j}{h}", tag=f"act{j}{h}", align_bytes=64)
+        def activate(j, h):
+            act = keep.tile([P, 2, P, 2], F32, name=f"act{j}{h}", tag=f"act{j}{h}", align_bytes=ALIGN)
             nc.scalar.activation(act[:], in_word_order(sums["w1", j, h][:]), GELU, bias=zero_bias[:])
             hidden[j, h] = keep.tile([P, 2, P, 2], BF16, name=f"hidden{j}{h}")
-            if split:
-                for u in range(2):
-                    nc.vector.tensor_tensor(hidden[j, h][:, u], in_word_order(sums["w3", j, h][:])[:, u], act[:, u], MULT)
-            else:
-                nc.vector.tensor_tensor(hidden[j, h][:], in_word_order(sums["w3", j, h][:]), act[:], MULT)
+            nc.vector.tensor_tensor(hidden[j, h][:], in_word_order(sums["w3", j, h][:]), act[:], MULT)
 
         h_words = {}
         h_mx = {}
 
-        def turn(units, b):
+        def turn(j, halves, b):
             turned = bank(b, "turned")[:].rearrange("p (g u c) -> p g u c", u=2, c=TILE)
-            for g, unit in enumerate(units):
-                pairs = hidden[unit][:].rearrange("c u p d -> c (u p d)").bitcast(F32)
+            for g, h in enumerate(halves):
+                pairs = hidden[j, h][:].rearrange("c u p d -> c (u p d)").bitcast(F32)
                 for u in range(2):
                     nc.tensor.transpose(turned[:, g, u, :], pairs[:, P * u : P * (u + 1)], ident[:])
-            j, h = units[0]
-            h_words[j, h] = keep.tile([P, len(units), TILE, 2], F32, name=f"h_words{j}{h}", align_bytes=64)
-            nc.scalar.copy(h_words[j, h][:], turned[:, 0 : len(units)].rearrange("p g u c -> p g c u"))
+            moved = keep.tile([P, len(halves), TILE, 2], F32, name=f"h_words{j}{halves[0]}", align_bytes=ALIGN)
+            nc.scalar.copy(moved[:], turned[:, 0 : len(halves)].rearrange("p g u c -> p g c u"))
+            h_words[j, halves] = moved
 
-        def quantize_h(units):
-            j, h = units[0]
-            source = h_words[j, h][:].rearrange("p g c u -> p (g c u)").bitcast(BF16)
-            for unit, operand in zip(units, quantize(source, len(units), f"h{j}{h}")):
-                h_mx[unit] = operand
+        def quantize_h(j, halves):
+            source = h_words[j, halves][:].rearrange("p g c u -> p (g c u)").bitcast(BF16)
+            name = f"h{j}{halves[0]}"
+            for h, operand in zip(halves, quantize(source, len(halves), name, name + "_codes")):
+                h_mx[j, h] = operand
 
         results = {}
 
@@ -276,72 +246,76 @@ def tile_moe_pre_glu_gelu_kernel(
             nc.scalar.copy(results[j][:], y[:, 0:TILE])
 
         def scatter(j):
-            lists = offsets[:, j * TILE // 16 : (j + 1) * TILE // 16]
-            nc.vector.tensor_copy(window[:].indirect(lists), results[j][:])
+            nc.vector.tensor_copy(window[:].indirect(list_of((j,))), results[j][:])
 
-        early = [(0, 0), (0, 1), (1, 0), (1, 1)]
+        both = tuple(range(HALVES))
 
-        gather((0, 1), 0, "gathered00")
-        for j in (0, 1):
-            x_bf = woven(1, f"x_bf{j}0", f"x_bf{j}0")
-            weave(x_bf[:, 0], j, 0)
-            quantize_x(x_bf, [(j, 0)])
-        for pair, (j, h) in enumerate(early):
-            open_sums(j, h, 2 * pair, 2 * pair + 1)
+        expert0_tiles = tuple(range(TILES_PER_EXPERT))
+        expert0_units = [(j, h) for j in expert0_tiles for h in both]
+
+        def prepare_expert0(s):
+            gather(expert0_tiles, s, f"gathered0{s}")
+            for j in expert0_tiles:
+                x_bf = woven(1, f"x_bf{j}{s}", f"x_bf{j}{s}")
+                weave(x_bf[:, 0], j, s)
+                quantize_x(x_bf, j, (s,), f"x{j}{s}_codes")
+
+        prepare_expert0(0)
+        for n, (j, h) in enumerate(expert0_units):
+            sums["w1", j, h] = bank(2 * n, f"a{j}{h}")
+            sums["w3", j, h] = bank(2 * n + 1, f"b{j}{h}")
         for m in first:
-            for j, h in early:
-                first_layer(j, h, 0, (m,))
-        gather((0, 1), 1, "gathered01")
-        for j in (0, 1):
-            x_bf = woven(1, f"x_bf{j}1", f"x_bf{j}1")
-            weave(x_bf[:, 0], j, 1)
-            quantize_x(x_bf, [(j, 1)])
-        for j, h in early:
-            first_layer(j, h, 1, first)
-        x_bf2 = woven(2, "x_bf2", "x_bf2")
+            for j, h in expert0_units:
+                first_layer(j, h, 0, m)
+        prepare_expert0(1)
+        for j, h in expert0_units:
+            for m in first:
+                first_layer(j, h, 1, m)
+
+        x_bf2 = woven(PASSES, "x_bf2", "x_bf2")
         x_bf30 = woven(1, "x_bf30", "x_bf30")
         gather((2, 3), 0, "gathered20")
         weave(x_bf2[:, 0], 2, 0)
         weave(x_bf30[:, 0], 3, 0)
         gather((2,), 1, "gate0")
         weave(x_bf2[:, 1], 2, 1)
-        quantize_x(x_bf2, [(2, 0), (2, 1)])
-        gather((3,), 1, "x_bf01")
-        quantize_x(x_bf30, [(3, 0)], "x_bf11")
-        activate(0, 0)
-        activate(0, 1)
-        activate(1, 0)
+        quantize_x(x_bf2, 2, (0, 1), "x20_codes")
+        gather((3,), 1, "gathered01")
+        quantize_x(x_bf30, 3, (0,), "x_bf11")
+        for j, h in expert0_units[:-1]:
+            activate(j, h)
         x_bf31 = woven(1, "x_bf31", "act00")
         weave(x_bf31[:, 0], 3, 1)
-        activate(1, 1)
-        quantize_x(x_bf31, [(3, 1)])
+        activate(*expert0_units[-1])
+        quantize_x(x_bf31, 3, (1,), "x31_codes")
+
         both_passes(2, 0, "w1", 0)
         both_passes(2, 1, "w1", 2)
         both_passes(2, 0, "w3", 1)
+        turn(0, both, 6)
         both_passes(2, 1, "w3", 3)
         activate(2, 0)
-        turn(early[0:2], 0)
+        quantize_h(0, both)
         both_passes(3, 0, "w1", 4)
         activate(2, 1)
+        turn(1, both, 0)
         both_passes(3, 0, "w3", 5)
-        quantize_h(early[0:2])
-        turn(early[2:4], 2)
-        both_passes(3, 1, "w1", 6)
-        activate(3, 0)
-        both_passes(3, 1, "w3", 7)
         second_layer(0, 1)
-        activate(3, 1)
-        quantize_h(early[2:4])
-        turn([(2, 0), (2, 1)], 3)
+        both_passes(3, 1, "w1", 2)
+        activate(3, 0)
+        quantize_h(1, both)
         scatter(0)
-        second_layer(1, 4)
-        quantize_h([(2, 0), (2, 1)])
-        turn([(3, 0)], 5)
-        turn([(3, 1)], 7)
-        second_layer(2, 6)
+        turn(2, both, 3)
+        both_passes(3, 1, "w3", 7)
+        second_layer(1, 6)
+        activate(3, 1)
+        quantize_h(2, both)
+        turn(3, (0,), 5)
         scatter(1)
-        quantize_h([(3, 0)])
-        quantize_h([(3, 1)])
+        turn(3, (1,), 7)
+        second_layer(2, 4)
+        quantize_h(3, (0,))
+        quantize_h(3, (1,))
         scatter(2)
         second_layer(3, 0)
         scatter(3)

from contextlib import ExitStack

import concourse.mybir as mybir
from concourse.masks import make_identity

K, T, E, C, H, N = 1024, 640, 2, 256, 1024, 128
FLOPS = 2 * E * C * (2 * K * H + H * N)

F32 = mybir.dt.float32
BF16 = mybir.dt.bfloat16
I32 = mybir.dt.int32
U32 = mybir.dt.uint32
U16 = mybir.dt.uint16
U8 = mybir.dt.uint8
FP8X4 = mybir.dt.float8_e4m3fn_x4
FP4X4 = mybir.dt.float4_e2m1fn_x4
MULT = mybir.AluOpType.mult
GELU = mybir.ActivationFunctionType.Gelu_apprx_tanh

P = 128
PACK = 4
PASS = P * PACK
PASSES = K // PASS
HALVES = H // PASS
TILE = 128
TILES_PER_EXPERT = C // TILE
QUADRANT = 32
SCALE_ROWS = 4
FP4_BYTES = 2
PER_COLUMN = 16
ALIGN = 64


def tile_moe_pre_glu_gelu_kernel(
    tc, xT, w1_words, w1_scales, w3_words, w3_scales, w2_words, w2_scales, gate, offs, out
):
    nc = tc.nc
    with ExitStack() as ctx:
        keep = ctx.enter_context(tc.tile_pool(name="keep", bufs=1))
        psum = ctx.enter_context(tc.psum_pool(name="psum", bufs=1))

        first = {"w1": (w1_words, w1_scales), "w3": (w3_words, w3_scales)}
        x_rows = xT.rearrange("(s p t) w -> s t p w", p=P, t=PACK)

        offsets = keep.tile([P, E * C // PER_COLUMN], U16, name="offsets")
        zero_in = keep.tile([P, 1], F32, name="zero_in")
        zero_bias = keep.tile([P, 1], F32, name="zero_bias")
        ident = keep.tile([P, P], F32, name="ident")
        window = keep.tile([P, T], F32, name="window")
        planes = {
            (m, e): keep.tile([P, PASSES, H], U8, name=f"{m}_plane{e}", align_bytes=ALIGN)
            for m in first
            for e in range(E)
        }
        w2_plane = keep.tile([P, E * HALVES, N], U8, name="w2_plane", align_bytes=ALIGN)
        w2_codes = keep.tile([P, E * HALVES, FP4_BYTES * N], U8, name="w2_codes", align_bytes=ALIGN)

        nc.vector.memset(zero_in[:], 0.0)
        for e in reversed(range(E)):
            for m in first:
                nc.vector.memset(planes[m, e][:].bitcast(I32), 0)
        make_identity(nc, ident[:])
        nc.gpsimd.memset(w2_plane[:].bitcast(I32), 0)
        nc.gpsimd.memset(window[:], 0.0)
        nc.scalar.activation(zero_bias[:], zero_in[:], GELU)

        def bank(b, name):
            return psum.tile([P, PASS], F32, name=name, tag=f"bank{b}")

        x_planes = {}
        gates = {}
        words = {}

        def load_x(s, t):
            x_planes[s, t] = keep.tile([P, T], F32, name=f"x{s}{t}")
            nc.sync.dma_start(x_planes[s, t][:], x_rows[s, t])

        def load_gate(e):
            gates[e] = keep.tile([P, C], F32, name=f"gate{e * TILES_PER_EXPERT}", align_bytes=ALIGN)
            nc.sync.dma_start(gates[e][:], gate[0:P, e * C : (e + 1) * C])

        def spread_gate(e, b):
            column = keep.tile([P, TILES_PER_EXPERT], F32, name="gate_column")
            row = gate[0, e * C : (e + 1) * C]
            nc.sync.dma_start(column[:], row.rearrange("(p c) -> p c", c=TILES_PER_EXPERT))
            spread = psum.tile([P, TILES_PER_EXPERT, P], F32, name="spread", tag=f"bank{b}")
            for c in range(TILES_PER_EXPERT):
                nc.tensor.transpose(spread[:, c, :], column[:, c : c + 1].to_broadcast([P, P]), ident[:])
            gates[e] = keep.tile([P, C], F32, name=f"gate{e * TILES_PER_EXPERT}", align_bytes=ALIGN)
            nc.scalar.copy(
                gates[e][:].rearrange("f (p c) -> f p c", c=TILES_PER_EXPERT), spread[:].rearrange("f c p -> f p c")
            )

        def load_scales(queue, plane, rows):
            for r in range(SCALE_ROWS):
                queue.dma_start(plane[r:P:QUADRANT].bitcast(I32), rows[r].bitcast(I32))

        def load_first_scales(queue, m, e):
            load_scales(queue, planes[m, e], first[m][1][e].rearrange("s (q r) n -> r q s n", r=SCALE_ROWS))

        def half_bytes(h):
            return slice(FP4_BYTES * PASS * h, FP4_BYTES * PASS * (h + 1))

        def load_words_of_pass(m, e, s):
            codes = keep.tile([P, FP4_BYTES * H], U8, name=f"{m}_codes{e}_pass{s}", align_bytes=ALIGN)
            nc.sync.dma_start(codes[:].bitcast(I32), first[m][0][e, s].bitcast(I32))
            for h in range(HALVES):
                words[m, e, s, h] = codes[:, half_bytes(h)]

        def load_words_of_expert(m, e):
            codes = keep.tile([P, PASSES, FP4_BYTES * H], U8, name=f"{m}_codes{e}", align_bytes=ALIGN)
            nc.sync.dma_start(codes[:].bitcast(I32), first[m][0][e].rearrange("s p n -> p s n").bitcast(I32))
            for s in range(PASSES):
                for h in range(HALVES):
                    words[m, e, s, h] = codes[:, s, half_bytes(h)]

        load_x(0, 0)
        load_gate(0)
        nc.sync.dma_start(offsets[:], offs)
        spread_gate(1, 7)
        for t in range(1, PACK):
            load_x(0, t)
        for t in range(PACK // 2):
            load_x(1, t)
        load_words_of_pass("w1", 0, 0)
        for t in range(PACK // 2, PACK):
            load_x(1, t)
        for m in first:
            load_first_scales(nc.sync, m, 0)
        load_words_of_pass("w3", 0, 0)
        for m in first:
            load_words_of_pass(m, 0, 1)
        for m in first:
            load_words_of_expert(m, 1)
        nc.sync.dma_start(w2_codes[:].bitcast(I32), w2_words.rearrange("e s p n -> p (e s) n").bitcast(I32))
        load_scales(nc.sync, w2_plane, w2_scales.rearrange("e s (q r) n -> r q (e s) n", r=SCALE_ROWS))
        for m in first:
            load_first_scales(nc.gpsimd, m, 1)

        def list_of(tiles):
            return offsets[:, tiles[0] * TILE // PER_COLUMN : (tiles[-1] + 1) * TILE // PER_COLUMN]

        gathered = {}

        def gather(tiles, s, tag):
            e, c0 = divmod(tiles[0] * TILE, C)
            width = len(tiles) * TILE
            values = keep.tile([P, PACK, width], F32, name=f"gathered{tiles[0]}{s}", tag=tag, align_bytes=ALIGN)
            for t in range(PACK):
                nc.vector.tensor_tensor(
                    values[:, t, :], x_planes[s, t][:].indirect(list_of(tiles)), gates[e][:, c0 : c0 + width], MULT
                )
            for n, j in enumerate(tiles):
                gathered[j, s] = values[:, :, n * TILE : (n + 1) * TILE]

        def woven(parts, name, tag):
            return keep.tile([P, parts, TILE, PACK], BF16, name=name, tag=tag, align_bytes=ALIGN)

        def weave(into, j, s):
            nc.scalar.copy(into, gathered[j, s].rearrange("p t c -> p c t"))

        def quantize(source, parts, name, tag):
            codes = keep.tile([P, parts, TILE], U32, name=name + "_codes", tag=tag, align_bytes=ALIGN)
            scales = keep.tile([P, parts, TILE], U8, name=name + "_scales", align_bytes=ALIGN)
            nc.vector.quantize_mx(
                out=codes[:].rearrange("p g c -> p (g c)").bitcast(FP8X4),
                scales=scales[:].rearrange("p g c -> p (g c)"),
                in_=source,
            )
            return [(codes[:, g, :], scales[:, g, :]) for g in range(parts)]

        x_mx = {}

        def quantize_x(source, j, passes, tag):
            flat = source[:].rearrange("p g c t -> p (g c t)")
            for s, operand in zip(passes, quantize(flat, len(passes), f"x{j}{passes[0]}", tag)):
                x_mx[j, s] = operand

        sums = {}

        def first_layer(j, h, s, m):
            e = j // TILES_PER_EXPERT
            codes, scales = x_mx[j, s]
            nc.tensor.matmul_mx(
                out=sums[m, j, h][:],
                lhsT=codes.bitcast(FP8X4),
                lhsT_scale=scales,
                rhs=words[m, e, s, h].bitcast(FP4X4),
                rhs_scale=planes[m, e][:, s, PASS * h : PASS * (h + 1)],
                start=(s == 0),
                stop=(s == PASSES - 1),
            )

        def both_passes(j, h, m, b):
            sums[m, j, h] = bank(b, f"{m}_sum{j}{h}")
            for s in range(PASSES):
                first_layer(j, h, s, m)

        hidden = {}

        def in_word_order(ap):
            return ap.rearrange("c (p u d) -> c u p d", u=2, d=2)

        def activate(j, h):
            act = keep.tile([P, 2, P, 2], F32, name=f"act{j}{h}", tag=f"act{j}{h}", align_bytes=ALIGN)
            nc.scalar.activation(act[:], in_word_order(sums["w1", j, h][:]), GELU, bias=zero_bias[:])
            hidden[j, h] = keep.tile([P, 2, P, 2], BF16, name=f"hidden{j}{h}")
            nc.vector.tensor_tensor(hidden[j, h][:], in_word_order(sums["w3", j, h][:]), act[:], MULT)

        h_words = {}
        h_mx = {}

        def turn(j, halves, b):
            turned = bank(b, "turned")[:].rearrange("p (g u c) -> p g u c", u=2, c=TILE)
            for g, h in enumerate(halves):
                pairs = hidden[j, h][:].rearrange("c u p d -> c (u p d)").bitcast(F32)
                for u in range(2):
                    nc.tensor.transpose(turned[:, g, u, :], pairs[:, P * u : P * (u + 1)], ident[:])
            moved = keep.tile([P, len(halves), TILE, 2], F32, name=f"h_words{j}{halves[0]}", align_bytes=ALIGN)
            nc.scalar.copy(moved[:], turned[:, 0 : len(halves)].rearrange("p g u c -> p g c u"))
            h_words[j, halves] = moved

        def quantize_h(j, halves):
            source = h_words[j, halves][:].rearrange("p g c u -> p (g c u)").bitcast(BF16)
            name = f"h{j}{halves[0]}"
            for h, operand in zip(halves, quantize(source, len(halves), name, name + "_codes")):
                h_mx[j, h] = operand

        results = {}

        def second_layer(j, b):
            e = j // TILES_PER_EXPERT
            y = bank(b, "y")
            for h in range(HALVES):
                codes, scales = h_mx[j, h]
                nc.tensor.matmul_mx(
                    out=y[:, 0:TILE],
                    lhsT=w2_codes[:, e * HALVES + h, :].bitcast(FP4X4),
                    lhsT_scale=w2_plane[:, e * HALVES + h, :],
                    rhs=codes.bitcast(FP8X4),
                    rhs_scale=scales,
                    start=(h == 0),
                    stop=(h == HALVES - 1),
                )
            results[j] = keep.tile([P, TILE], F32, name=f"result{j}")
            nc.scalar.copy(results[j][:], y[:, 0:TILE])

        def scatter(j):
            nc.vector.tensor_copy(window[:].indirect(list_of((j,))), results[j][:])

        both = tuple(range(HALVES))

        expert0_tiles = tuple(range(TILES_PER_EXPERT))
        expert0_units = [(j, h) for j in expert0_tiles for h in both]

        def prepare_expert0(s):
            gather(expert0_tiles, s, f"gathered0{s}")
            for j in expert0_tiles:
                x_bf = woven(1, f"x_bf{j}{s}", f"x_bf{j}{s}")
                weave(x_bf[:, 0], j, s)
                quantize_x(x_bf, j, (s,), f"x{j}{s}_codes")

        prepare_expert0(0)
        for n, (j, h) in enumerate(expert0_units):
            sums["w1", j, h] = bank(2 * n, f"a{j}{h}")
            sums["w3", j, h] = bank(2 * n + 1, f"b{j}{h}")
        for m in first:
            for j, h in expert0_units:
                first_layer(j, h, 0, m)
        prepare_expert0(1)
        for j, h in expert0_units:
            for m in first:
                first_layer(j, h, 1, m)

        x_bf2 = woven(PASSES, "x_bf2", "x_bf2")
        x_bf30 = woven(1, "x_bf30", "x_bf30")
        gather((2, 3), 0, "gathered20")
        weave(x_bf2[:, 0], 2, 0)
        weave(x_bf30[:, 0], 3, 0)
        gather((2,), 1, "gate0")
        weave(x_bf2[:, 1], 2, 1)
        quantize_x(x_bf2, 2, (0, 1), "x20_codes")
        gather((3,), 1, "gathered01")
        quantize_x(x_bf30, 3, (0,), "x_bf11")
        for j, h in expert0_units[:-1]:
            activate(j, h)
        x_bf31 = woven(1, "x_bf31", "act00")
        weave(x_bf31[:, 0], 3, 1)
        activate(*expert0_units[-1])
        quantize_x(x_bf31, 3, (1,), "x31_codes")

        both_passes(2, 0, "w1", 0)
        both_passes(2, 1, "w1", 2)
        both_passes(2, 0, "w3", 1)
        turn(0, both, 6)
        both_passes(2, 1, "w3", 3)
        activate(2, 0)
        quantize_h(0, both)
        both_passes(3, 0, "w1", 4)
        activate(2, 1)
        turn(1, both, 0)
        both_passes(3, 0, "w3", 5)
        second_layer(0, 1)
        both_passes(3, 1, "w1", 2)
        activate(3, 0)
        quantize_h(1, both)
        scatter(0)
        turn(2, both, 3)
        both_passes(3, 1, "w3", 7)
        second_layer(1, 6)
        activate(3, 1)
        quantize_h(2, both)
        turn(3, (0,), 5)
        scatter(1)
        turn(3, (1,), 7)
        second_layer(2, 4)
        quantize_h(3, (0,))
        quantize_h(3, (1,))
        scatter(2)
        second_layer(3, 0)
        scatter(3)
        nc.sync.dma_start(out, window[:])
